import numpy as np, ml_dtypes
CORES = [51,54,179,182]
N = 4
TK = 128
def setup_inputs(rng):
    return {"x": rng.standard_normal((N, 128, TK), dtype=np.float32).astype(ml_dtypes.bfloat16), "w1": (rng.standard_normal((N, 128, 128), dtype=np.float32) / 8).astype(ml_dtypes.bfloat16), "w2": (rng.standard_normal((N, 128, 128), dtype=np.float32) / 8).astype(ml_dtypes.bfloat16)}
def setup_inputs_big(rng):
    d = setup_inputs(rng)
    for k in ("x", "w1", "w2"): d[k] = (d[k].astype(np.float32) * 1024.0).astype(d[k].dtype)
    return d
def setup_inputs_small(rng):
    d = setup_inputs(rng)
    for k in ("x", "w1", "w2"): d[k] = (d[k].astype(np.float32) * (1 / 1024.0)).astype(d[k].dtype)
    return d
def setup_inputs_apart(rng):
    d = setup_inputs(rng)
    f = (10.0 ** rng.permutation(np.linspace(-1.5, 1.5, N))).astype(np.float32).reshape(N, 1, 1)
    for k in ("x", "w1", "w2"): d[k] = (d[k].astype(np.float32) * f).astype(d[k].dtype)
    return d
def reference(x, w1, w2):
    X, W1, W2 = x.astype(np.float64), w1.astype(np.float64), w2.astype(np.float64)
    y = np.zeros((N, 128, TK))
    for r in range(N):
        for j in range(N):
            y[r] += W2[j].T @ np.maximum(W1[j].T @ X[r], 0.0)
    return {"y": y.astype(ml_dtypes.bfloat16 if x.dtype != np.float64 else np.float64)}

@@ -1,0 +1,127 @@
+from concourse.bass import DstId, RemoteDMATransfer
+from concourse.mybir import AluOpType
+
+N = 4
+D = 128
+W = 2 * D
+
+SCRATCH = {
+    "wall": ("sbuf", [128, N * W], "bfloat16"),
+    "xs": ("sbuf", [128, D], "bfloat16"),
+    "zero": ("sbuf", [128, D], "float32"),
+    "hs": ("sbuf", [128, N * D], "bfloat16"),
+    "ys": ("sbuf", [128, D], "bfloat16"),
+    "ph0": ("psum", [128, 512], "float32"),
+    "ph1": ("psum", [128, 512], "float32"),
+    "ph2": ("psum", [128, 512], "float32"),
+    "ph3": ("psum", [128, 512], "float32"),
+    "py": ("psum", [128, 512], "float32"),
+}
+SEMAPHORES = (["wld", "xld", "sent", "zs", "m2", "yc", "st"]
+              + ["arr%d" % j for j in range(N)] + ["m1_%d" % j for j in range(N)] + ["h%d" % j for j in range(N)])
+
+
+def _engines(mask):
+    return [1 << i for i in range(mask.bit_length()) if (mask >> i) & 1]
+
+
+def _join(bits):
+    m = 0
+    for b in bits:
+        m |= b
+    return m
+
+
+def _same_chip(topo, a, b):
+    return (topo.host(a), topo.chip(a)) == (topo.host(b), topo.chip(b))
+
+
+def _plan(topo, cores, src):
+    far = [d for d in cores if d != src and not _same_chip(topo, src, d)]
+    near = [d for d in cores if d != src and _same_chip(topo, src, d)]
+    far_mask = 0
+    far_plan = []
+    if far:
+        far_mask = topo.mask(src, far[0])
+        for d in far:
+            far_mask &= topo.mask(src, d)
+        eng = _engines(far_mask)
+        share = len(eng) // len(far)
+        far_plan = [(d, _join(eng[k * share:(k + 1) * share])) for k, d in enumerate(far)]
+    near_plan = []
+    if near:
+        free = topo.mask(src, near[0]) & ~far_mask
+        eng = _engines(free)
+        share = len(eng) // len(near)
+        near_plan = [(d, _join(eng[k * share:(k + 1) * share])) for k, d in enumerate(near)]
+    return far_plan, near_plan
+
+
+def rank_program(g, core, T, topo):
+    rank = T.rank_of(core)
+    if rank is None:
+        return
+    cores = list(T.cores)
+
+    def slot(j):
+        return T.wall[:, j * W:(j + 1) * W]
+
+    g.sync.dma_start(T.wall[:, rank * W:rank * W + D], T.w1[:, :]).then_inc(T.sem.wld, 16)
+    g.scalar.dma_start(T.wall[:, rank * W + D:(rank + 1) * W], T.w2[:, :]).then_inc(T.sem.wld, 16)
+    g.sync.dma_start(T.xs[:, :], T.x[:, :]).then_inc(T.sem.xld, 16)
+    g.vector.memset(T.zero[:, :], 0.0).then_inc(T.sem.zs, 1)
+
+    far_plan, near_plan = _plan(topo, cores, core)
+    g.wait_ge(T.sem.wld, 32)
+    sent = 0
+    for plan in (far_plan, near_plan):
+        if not plan:
+            continue
+        transfers = []
+        for d, m in plan:
+            rid, pid = topo.addr(d, core)
+            transfers.append(RemoteDMATransfer(dst_ids=[DstId(rid=rid, pnc=pid)], dma_engine_mask=m,
+                                               remote_sem=T.sem["arr%d" % rank], src=slot(rank), dst=slot(rank)))
+            sent += len(_engines(m))
+        g.remote_dma_fused(transfers, local_sem=T.sem.sent)
+
+    def arrives(j):
+        fp, np_ = _plan(topo, cores, cores[j])
+        return len(_engines(dict(fp + np_)[core]))
+
+    others = [j for j in range(N) if j != rank]
+    others.sort(key=lambda j: (not _same_chip(topo, cores[j], core), topo.die(cores[j]) != topo.die(core)))
+    order = [rank] + others
+
+    def mm1(j):
+        if j == rank:
+            g.tensor.wait_ge(T.sem.wld, 32)
+            g.tensor.wait_ge(T.sem.xld, 16)
+        else:
+            g.tensor.wait_ge(T.sem["arr%d" % j], arrives(j))
+        g.tensor.matmul(T["ph%d" % j][:, 0:D], T.wall[:, j * W:j * W + D], T.xs[:, :],
+                        start=True, stop=True).then_inc(T.sem["m1_%d" % j], 1)
+
+    def mm2(j):
+        g.tensor.wait_ge(T.sem["h%d" % j], 1)
+        g.tensor.matmul(T.py[:, 0:D], T.wall[:, j * W + D:(j + 1) * W], T.hs[:, j * D:(j + 1) * D],
+                        start=(j == order[0]), stop=(j == order[-1])).then_inc(T.sem.m2, 1)
+
+    mm1(order[0]); mm2(order[0])
+    mm1(order[1]); mm2(order[1])
+    mm1(order[2]); mm1(order[3])
+    mm2(order[2]); mm2(order[3])
+
+    g.vector.wait_ge(T.sem.zs, 1)
+    for j in order:
+        g.vector.wait_ge(T.sem["m1_%d" % j], 1)
+        g.vector.tensor_tensor(out=T.hs[:, j * D:(j + 1) * D], in0=T["ph%d" % j][:, 0:D], in1=T.zero[:, :],
+                               op=AluOpType.max).then_inc(T.sem["h%d" % j], 1)
+    g.vector.wait_ge(T.sem.m2, N)
+    g.vector.tensor_copy(out=T.ys[:, :], in_=T.py[:, 0:D]).then_inc(T.sem.yc, 1)
+
+    g.sync.wait_ge(T.sem.yc, 1)
+    g.sync.dma_start(T.y[:, :], T.ys[:, :]).then_inc(T.sem.st, 16)
+
+    g.wait_ge(T.sem.sent, sent)
+    g.wait_ge(T.sem.st, 16)

@@ -1,9 +1,10 @@
 from concourse.bass import DstId, RemoteDMATransfer
-from concourse.mybir import AluOpType
+from concourse.mybir import AluOpType, ActivationFunctionType
 
 N = 4
 D = 128
 W = 2 * D
+H = D // 2
 
 SCRATCH = {
     "wall": ("sbuf", [128, N * W], "bfloat16"),
@@ -15,10 +16,12 @@ SCRATCH = {
     "ph1": ("psum", [128, 512], "float32"),
     "ph2": ("psum", [128, 512], "float32"),
     "ph3": ("psum", [128, 512], "float32"),
-    "py": ("psum", [128, 512], "float32"),
+    "pya": ("psum", [128, 512], "float32"),
+    "pyb": ("psum", [128, 512], "float32"),
 }
-SEMAPHORES = (["wld", "xld", "sent", "zs", "m2", "yc", "st"]
-              + ["arr%d" % j for j in range(N)] + ["m1_%d" % j for j in range(N)] + ["h%d" % j for j in range(N)])
+SEMAPHORES = (["w1ld", "w2ld", "xld", "sent", "zs", "m2a", "m2b", "yc", "st"]
+              + ["arr%d" % j for j in range(N)] + ["brr%d" % j for j in range(N)]
+              + ["m1_%d" % j for j in range(N)] + ["h%d" % j for j in range(N)])
 
 
 def _engines(mask):
@@ -57,71 +60,109 @@ def _plan(topo, cores, src):
     return far_plan, near_plan
 
 
+def _turns(topo, cores, src):
+    far_plan, _ = _plan(topo, cores, src)
+    whole = _join([m for _, m in far_plan])
+    dsts = sorted([d for d, _ in far_plan], key=lambda d: topo.die(d) == topo.die(src))
+    return [(d, whole) for d in dsts]
+
+
 def rank_program(g, core, T, topo):
     rank = T.rank_of(core)
     if rank is None:
         return
     cores = list(T.cores)
 
+    def w1_of(j):
+        return T.wall[:, j * W:j * W + D]
+
+    def w2_of(j):
+        return T.wall[:, j * W + D:(j + 1) * W]
+
     def slot(j):
         return T.wall[:, j * W:(j + 1) * W]
 
-    g.sync.dma_start(T.wall[:, rank * W:rank * W + D], T.w1[:, :]).then_inc(T.sem.wld, 16)
-    g.scalar.dma_start(T.wall[:, rank * W + D:(rank + 1) * W], T.w2[:, :]).then_inc(T.sem.wld, 16)
+    g.sync.dma_start(w1_of(rank), T.w1[:, :]).then_inc(T.sem.w1ld, 16)
+    g.scalar.dma_start(w2_of(rank), T.w2[:, :]).then_inc(T.sem.w2ld, 16)
     g.sync.dma_start(T.xs[:, :], T.x[:, :]).then_inc(T.sem.xld, 16)
     g.vector.memset(T.zero[:, :], 0.0).then_inc(T.sem.zs, 1)
 
     far_plan, near_plan = _plan(topo, cores, core)
-    g.wait_ge(T.sem.wld, 32)
-    sent = 0
-    for plan in (far_plan, near_plan):
+    sent = [0]
+
+    def send(plan, ap, sem):
         if not plan:
-            continue
+            return
         transfers = []
         for d, m in plan:
             rid, pid = topo.addr(d, core)
             transfers.append(RemoteDMATransfer(dst_ids=[DstId(rid=rid, pnc=pid)], dma_engine_mask=m,
-                                               remote_sem=T.sem["arr%d" % rank], src=slot(rank), dst=slot(rank)))
-            sent += len(_engines(m))
+                                               remote_sem=sem, src=ap, dst=ap))
+            sent[0] += len(_engines(m))
         g.remote_dma_fused(transfers, local_sem=T.sem.sent)
+
+    g.wait_ge(T.sem.w1ld, 16)
+    send(far_plan, w1_of(rank), T.sem["arr%d" % rank])
+    g.wait_ge(T.sem.w2ld, 16)
+    turn = _turns(topo, cores, core)
+    send(turn[:1], w2_of(rank), T.sem["brr%d" % rank])
+    send(near_plan, slot(rank), T.sem["arr%d" % rank])
+    send(turn[1:], w2_of(rank), T.sem["brr%d" % rank])
 
     def arrives(j):
         fp, np_ = _plan(topo, cores, cores[j])
         return len(_engines(dict(fp + np_)[core]))
 
-    others = [j for j in range(N) if j != rank]
-    others.sort(key=lambda j: (not _same_chip(topo, cores[j], core), topo.die(cores[j]) != topo.die(core)))
-    order = [rank] + others
+    def arrives2(j):
+        return len(_engines(dict(_turns(topo, cores, cores[j]))[core]))
+
+    near = [j for j in range(N) if j != rank and _same_chip(topo, cores[j], core)]
+    far = [j for j in range(N) if j != rank and not _same_chip(topo, cores[j], core)]
+    far.sort(key=lambda j: topo.die(cores[j]) != topo.die(core))
+    far2 = sorted(far, key=lambda j: [d for d, _ in _turns(topo, cores, cores[j])].index(core))
+    order2 = [rank] + near + far2
 
     def mm1(j):
         if j == rank:
-            g.tensor.wait_ge(T.sem.wld, 32)
+            g.tensor.wait_ge(T.sem.w1ld, 16)
             g.tensor.wait_ge(T.sem.xld, 16)
         else:
             g.tensor.wait_ge(T.sem["arr%d" % j], arrives(j))
-        g.tensor.matmul(T["ph%d" % j][:, 0:D], T.wall[:, j * W:j * W + D], T.xs[:, :],
+        g.tensor.matmul(T["ph%d" % j][:, 0:D], w1_of(j), T.xs[:, :],
                         start=True, stop=True).then_inc(T.sem["m1_%d" % j], 1)
 
     def mm2(j):
+        if j == rank:
+            g.tensor.wait_ge(T.sem.w2ld, 16)
+        elif j in far:
+            g.tensor.wait_ge(T.sem["brr%d" % j], arrives2(j))
         g.tensor.wait_ge(T.sem["h%d" % j], 1)
-        g.tensor.matmul(T.py[:, 0:D], T.wall[:, j * W + D:(j + 1) * W], T.hs[:, j * D:(j + 1) * D],
-                        start=(j == order[0]), stop=(j == order[-1])).then_inc(T.sem.m2, 1)
+        first, last = (j == order2[0]), (j == order2[-1])
+        g.tensor.matmul(T.pya[:, 0:H], w2_of(j), T.hs[:, j * D:j * D + H],
+                        start=first, stop=last).then_inc(T.sem.m2a, 1)
+        g.tensor.matmul(T.pyb[:, 0:H], w2_of(j), T.hs[:, j * D + H:(j + 1) * D],
+                        start=first, stop=last).then_inc(T.sem.m2b, 1)
 
-    mm1(order[0]); mm2(order[0])
-    mm1(order[1]); mm2(order[1])
-    mm1(order[2]); mm1(order[3])
-    mm2(order[2]); mm2(order[3])
+    mm1(rank); mm2(rank)
+    for j in far:
+        mm1(j)
+    for j in near:
+        mm1(j); mm2(j)
+    for j in far2:
+        mm2(j)
 
     g.vector.wait_ge(T.sem.zs, 1)
-    for j in order:
+    for j in [rank] + far + near:
         g.vector.wait_ge(T.sem["m1_%d" % j], 1)
         g.vector.tensor_tensor(out=T.hs[:, j * D:(j + 1) * D], in0=T["ph%d" % j][:, 0:D], in1=T.zero[:, :],
                                op=AluOpType.max).then_inc(T.sem["h%d" % j], 1)
-    g.vector.wait_ge(T.sem.m2, N)
-    g.vector.tensor_copy(out=T.ys[:, :], in_=T.py[:, 0:D]).then_inc(T.sem.yc, 1)
+    g.vector.wait_ge(T.sem.m2a, N)
+    g.vector.tensor_copy(out=T.ys[:, 0:H], in_=T.pya[:, 0:H]).then_inc(T.sem.yc, 1)
+    g.scalar.wait_ge(T.sem.m2b, N)
+    g.scalar.activation(T.ys[:, H:D], T.pyb[:, 0:H], ActivationFunctionType.Copy).then_inc(T.sem.yc, 1)
 
-    g.sync.wait_ge(T.sem.yc, 1)
+    g.sync.wait_ge(T.sem.yc, 2)
     g.sync.dma_start(T.y[:, :], T.ys[:, :]).then_inc(T.sem.st, 16)
 
-    g.wait_ge(T.sem.sent, sent)
+    g.wait_ge(T.sem.sent, sent[0])
     g.wait_ge(T.sem.st, 16)

from concourse.bass import DstId, RemoteDMATransfer
from concourse.mybir import AluOpType, ActivationFunctionType

N = 4
D = 128
W = 2 * D
H = D // 2

SCRATCH = {
    "wall": ("sbuf", [128, N * W], "bfloat16"),
    "xs": ("sbuf", [128, D], "bfloat16"),
    "zero": ("sbuf", [128, D], "float32"),
    "hs": ("sbuf", [128, N * D], "bfloat16"),
    "ys": ("sbuf", [128, D], "bfloat16"),
    "ph0": ("psum", [128, 512], "float32"),
    "ph1": ("psum", [128, 512], "float32"),
    "ph2": ("psum", [128, 512], "float32"),
    "ph3": ("psum", [128, 512], "float32"),
    "pya": ("psum", [128, 512], "float32"),
    "pyb": ("psum", [128, 512], "float32"),
}
SEMAPHORES = (["w1ld", "w2ld", "xld", "sent", "zs", "m2a", "m2b", "yc", "st"]
              + ["arr%d" % j for j in range(N)] + ["brr%d" % j for j in range(N)]
              + ["m1_%d" % j for j in range(N)] + ["h%d" % j for j in range(N)])


def _engines(mask):
    return [1 << i for i in range(mask.bit_length()) if (mask >> i) & 1]


def _join(bits):
    m = 0
    for b in bits:
        m |= b
    return m


def _same_chip(topo, a, b):
    return (topo.host(a), topo.chip(a)) == (topo.host(b), topo.chip(b))


def _plan(topo, cores, src):
    far = [d for d in cores if d != src and not _same_chip(topo, src, d)]
    near = [d for d in cores if d != src and _same_chip(topo, src, d)]
    far_mask = 0
    far_plan = []
    if far:
        far_mask = topo.mask(src, far[0])
        for d in far:
            far_mask &= topo.mask(src, d)
        eng = _engines(far_mask)
        share = len(eng) // len(far)
        far_plan = [(d, _join(eng[k * share:(k + 1) * share])) for k, d in enumerate(far)]
    near_plan = []
    if near:
        free = topo.mask(src, near[0]) & ~far_mask
        eng = _engines(free)
        share = len(eng) // len(near)
        near_plan = [(d, _join(eng[k * share:(k + 1) * share])) for k, d in enumerate(near)]
    return far_plan, near_plan


def _turns(topo, cores, src):
    far_plan, _ = _plan(topo, cores, src)
    whole = _join([m for _, m in far_plan])
    dsts = sorted([d for d, _ in far_plan], key=lambda d: topo.die(d) == topo.die(src))
    return [(d, whole) for d in dsts]


def rank_program(g, core, T, topo):
    rank = T.rank_of(core)
    if rank is None:
        return
    cores = list(T.cores)

    def w1_of(j):
        return T.wall[:, j * W:j * W + D]

    def w2_of(j):
        return T.wall[:, j * W + D:(j + 1) * W]

    def slot(j):
        return T.wall[:, j * W:(j + 1) * W]

    g.sync.dma_start(w1_of(rank), T.w1[:, :]).then_inc(T.sem.w1ld, 16)
    g.scalar.dma_start(w2_of(rank), T.w2[:, :]).then_inc(T.sem.w2ld, 16)
    g.sync.dma_start(T.xs[:, :], T.x[:, :]).then_inc(T.sem.xld, 16)
    g.vector.memset(T.zero[:, :], 0.0).then_inc(T.sem.zs, 1)

    far_plan, near_plan = _plan(topo, cores, core)
    sent = [0]

    def send(plan, ap, sem):
        if not plan:
            return
        transfers = []
        for d, m in plan:
            rid, pid = topo.addr(d, core)
            transfers.append(RemoteDMATransfer(dst_ids=[DstId(rid=rid, pnc=pid)], dma_engine_mask=m,
                                               remote_sem=sem, src=ap, dst=ap))
            sent[0] += len(_engines(m))
        g.remote_dma_fused(transfers, local_sem=T.sem.sent)

    g.wait_ge(T.sem.w1ld, 16)
    send(far_plan, w1_of(rank), T.sem["arr%d" % rank])
    g.wait_ge(T.sem.w2ld, 16)
    turn = _turns(topo, cores, core)
    send(turn[:1], w2_of(rank), T.sem["brr%d" % rank])
    send(near_plan, slot(rank), T.sem["arr%d" % rank])
    send(turn[1:], w2_of(rank), T.sem["brr%d" % rank])

    def arrives(j):
        fp, np_ = _plan(topo, cores, cores[j])
        return len(_engines(dict(fp + np_)[core]))

    def arrives2(j):
        return len(_engines(dict(_turns(topo, cores, cores[j]))[core]))

    near = [j for j in range(N) if j != rank and _same_chip(topo, cores[j], core)]
    far = [j for j in range(N) if j != rank and not _same_chip(topo, cores[j], core)]
    far.sort(key=lambda j: topo.die(cores[j]) != topo.die(core))
    far2 = sorted(far, key=lambda j: [d for d, _ in _turns(topo, cores, cores[j])].index(core))
    order2 = [rank] + near + far2

    def mm1(j):
        if j == rank:
            g.tensor.wait_ge(T.sem.w1ld, 16)
            g.tensor.wait_ge(T.sem.xld, 16)
        else:
            g.tensor.wait_ge(T.sem["arr%d" % j], arrives(j))
        g.tensor.matmul(T["ph%d" % j][:, 0:D], w1_of(j), T.xs[:, :],
                        start=True, stop=True).then_inc(T.sem["m1_%d" % j], 1)

    def mm2(j):
        if j == rank:
            g.tensor.wait_ge(T.sem.w2ld, 16)
        elif j in far:
            g.tensor.wait_ge(T.sem["brr%d" % j], arrives2(j))
        g.tensor.wait_ge(T.sem["h%d" % j], 1)
        first, last = (j == order2[0]), (j == order2[-1])
        g.tensor.matmul(T.pya[:, 0:H], w2_of(j), T.hs[:, j * D:j * D + H],
                        start=first, stop=last).then_inc(T.sem.m2a, 1)
        g.tensor.matmul(T.pyb[:, 0:H], w2_of(j), T.hs[:, j * D + H:(j + 1) * D],
                        start=first, stop=last).then_inc(T.sem.m2b, 1)

    mm1(rank); mm2(rank)
    for j in far:
        mm1(j)
    for j in near:
        mm1(j); mm2(j)
    for j in far2:
        mm2(j)

    g.vector.wait_ge(T.sem.zs, 1)
    for j in [rank] + far + near:
        g.vector.wait_ge(T.sem["m1_%d" % j], 1)
        g.vector.tensor_tensor(out=T.hs[:, j * D:(j + 1) * D], in0=T["ph%d" % j][:, 0:D], in1=T.zero[:, :],
                               op=AluOpType.max).then_inc(T.sem["h%d" % j], 1)
    g.vector.wait_ge(T.sem.m2a, N)
    g.vector.tensor_copy(out=T.ys[:, 0:H], in_=T.pya[:, 0:H]).then_inc(T.sem.yc, 1)
    g.scalar.wait_ge(T.sem.m2b, N)
    g.scalar.activation(T.ys[:, H:D], T.pyb[:, 0:H], ActivationFunctionType.Copy).then_inc(T.sem.yc, 1)

    g.sync.wait_ge(T.sem.yc, 2)
    g.sync.dma_start(T.y[:, :], T.ys[:, :]).then_inc(T.sem.st, 16)

    g.wait_ge(T.sem.sent, sent[0])
    g.wait_ge(T.sem.st, 16)
